import numpy as np
import ml_dtypes


def mxq(x, axis, fmt="e4m3"):
    dtype, down = {"e4m3": (ml_dtypes.float8_e4m3fn, 7), "e5m2": (ml_dtypes.float8_e5m2, 14)}[fmt]
    v = np.moveaxis(np.asarray(x, np.float32).astype(ml_dtypes.bfloat16).astype(np.float64), axis, -1)
    blocks = v.reshape(v.shape[:-1] + (-1, 32))
    amax = np.abs(blocks).max(-1, keepdims=True)
    byte = np.maximum(np.where(amax > 0, np.frexp(amax)[1] - 1 + 127, 0) - down, 1)
    scale = np.exp2(byte - 127.0)
    codes = (blocks / scale).astype(np.float32).astype(dtype).astype(np.float64)
    return np.moveaxis((codes * scale).reshape(v.shape), -1, axis)


WIDE = False


def mx_kscale(k):
    if not WIDE:
        return np.ones(k)
    levels = np.array([10, -10, 5, -5, 0])
    if k % 512:
        return np.exp2(np.random.permutation(np.resize(levels, k // 32))).repeat(32)
    a = np.empty((k // 512, 16))
    for p in range(k // 512):
        a[p, :8] = np.random.permutation(np.resize(levels, 8))
        for g in range(8):
            far = levels[np.abs(levels - a[p, g]) >= 10]
            a[p, g + 8] = far[np.random.randint(len(far))]
    return np.exp2(a.ravel()).repeat(32)


def f64(x):
    return np.asarray(x).astype(np.float64)


def striped(idx):
    return np.tile(idx.reshape(-1, 16).T, (8, 1)).astype(np.uint16)


def unstriped(offs):
    return offs[:16].T.reshape(-1).astype(np.int64)


def pack_weight(w):
    k, n = w.shape
    w = f64(np.asarray(w, np.float32).astype(ml_dtypes.bfloat16)).reshape(k // 32, 32, n)
    amax = np.abs(w).max(1)
    byte = np.clip(np.where(amax > 0, np.frexp(amax)[1] - 1 + 127 - 7, 1), 1, 254)
    scaled = (w * np.exp2(127.0 - byte)[:, None, :]).reshape(k, n).astype(np.float32)
    words = np.ascontiguousarray(scaled.reshape(k // 512, 128, 4, n).transpose(0, 1, 3, 2)).astype(ml_dtypes.float8_e4m3fn).view(np.uint8)
    return words, np.ascontiguousarray(byte.astype(np.uint8).reshape(k // 512, 16, n))


def unpack_weight(words, scales):
    g, p, n, _ = words.shape
    vals = np.ascontiguousarray(words).view(ml_dtypes.float8_e4m3fn).astype(np.float64) * np.repeat(np.exp2(scales.astype(np.float64) - 127.0), 8, axis=1)[..., None]
    return vals.transpose(0, 1, 3, 2).reshape(g * 512, n)


K, T, E, C, N = 2048, 512, 2, 256, 256


def by_expert(wq, xq):
    return np.concatenate([wq[e].T @ xq[:, e * C:(e + 1) * C] for e in range(E)], axis=1)


def setup_inputs():
    n = np.random.standard_normal
    s = mx_kscale(K)[:, None]
    packed = [pack_weight(m) for m in n((E, K, N)) / np.sqrt(K) / s[None]]
    return {
        "xT": (n((K, T)) * s).astype(np.float32),
        "w_words": np.stack([m[0] for m in packed]),
        "w_scales": np.stack([m[1] for m in packed]),
        "gate": np.tile(np.random.uniform(0.2, 1.0, E * C), (N, 1)).astype(np.float32),
        "offs": striped(np.random.permutation(T)[:E * C]),
    }


def reference(xT, w_words, w_scales, gate, offs):
    idx = unstriped(offs)
    xq = mxq(f64(xT)[:, idx], 0, "e4m3")
    w = np.stack([unpack_weight(w_words[e], w_scales[e]) for e in range(E)])
    y = by_expert(w, xq)
    out = np.zeros((N, T))
    out[:, idx] = f64(gate) * y
    return out

@@ -1,0 +1,187 @@
+from contextlib import ExitStack
+
+import concourse.mybir as mybir
+
+K, T, E, C, N = 2048, 512, 2, 256, 256
+FLOPS = 2 * K * N * E * C
+
+F32 = mybir.dt.float32
+BF16 = mybir.dt.bfloat16
+U32 = mybir.dt.uint32
+I32 = mybir.dt.int32
+U16 = mybir.dt.uint16
+U8 = mybir.dt.uint8
+FP8X4 = mybir.dt.float8_e4m3fn_x4
+MULT = mybir.AluOpType.mult
+COPY = mybir.ActivationFunctionType.Copy
+
+P = 128
+PASSES = K // 512
+UNITS = 2 * PASSES
+NB = N // P
+S = E * C
+H = T // 2
+
+
+def tile_routed_moe_kernel(tc, xT, w_words, w_scales, gate, offs, out):
+    nc = tc.nc
+    with ExitStack() as ctx:
+        keep = ctx.enter_context(tc.tile_pool(name="keep", bufs=1))
+        psum = ctx.enter_context(tc.psum_pool(name="psum", bufs=1))
+
+        offs_t = keep.tile([P, S // 16], U16, name="offs_t")
+
+        warm_in = keep.tile([P, 1], F32, name="warm_in")
+        warm_out = keep.tile([P, 1], F32, name="warm_out")
+        nc.vector.memset(warm_in[:], 0.0)
+        nc.scalar.activation(warm_out[:], warm_in[:], COPY)
+
+        ws = keep.tile([P, E * PASSES, N], U8, name="ws", align_bytes=64)
+        nc.vector.memset(ws[:].rearrange("p c n -> p (c n)").bitcast(I32), 0)
+
+        xv = xT.rearrange("(g p t) n -> g p t n", p=P, t=4)
+        SPLIT = 2
+        LAST = UNITS - 1
+        raw = {}
+        for i in range(UNITS):
+            g, u = divmod(i, 2)
+            if i < SPLIT:
+                for b in range(2):
+                    raw[i, b] = keep.tile([P, 2, H], F32, name="raw%d_%d" % (i, b))
+                    nc.sync.dma_start(raw[i, b][:], xv[g, :, 2 * u : 2 * u + 2, b * H : (b + 1) * H])
+                if i == 0:
+                    nc.sync.dma_start(offs_t[:], offs)
+            else:
+                raw[i] = keep.tile([P, 2, T], F32, name="raw%d" % i)
+                nc.sync.dma_start(raw[i][:], xv[g, :, 2 * u : 2 * u + 2, :])
+
+        sv = w_scales.rearrange("e a q n -> (e a) q n").rearrange("c (Q r) n -> r Q c n", r=4)
+        for r in range(4):
+            nc.sync.dma_start(ws[r:P:32, :, :].bitcast(I32), sv[r].bitcast(I32))
+
+        wq = []
+        for a in range(PASSES):
+            wq_a = keep.tile([P, E, N], I32, name="wq%d" % a, align_bytes=64)
+            nc.sync.dma_start(wq_a[:], w_words[:, a].rearrange("e p n r -> p e (n r)").bitcast(I32))
+            wq.append(wq_a)
+
+        gt = []
+        for nb in range(NB):
+            gt_nb = keep.tile([P, S], F32, name="gt%d" % nb)
+            nc.sync.dma_start(gt_nb[:], gate[nb * P : (nb + 1) * P, :])
+            gt.append(gt_nb)
+
+        xc = keep.tile([P, PASSES, S], U32, name="xc", align_bytes=64)
+        xs = keep.tile([P, PASSES, S], U8, name="xs", align_bytes=64)
+        xi = [keep.tile([P, S, 4], BF16, name="xi%d" % g, align_bytes=64) for g in range(PASSES)]
+        win = keep.tile([P, LAST * T, 2], BF16, name="win", align_bytes=64)
+        winw = win[:].rearrange("p t e -> p (t e)").bitcast(U32)
+        planes = keep.tile([P, 2, T], BF16, name="planes", align_bytes=64)
+        xg = [keep.tile([P, 2, S, 2], BF16, name="xg%d" % g, align_bytes=64) for g in range(PASSES - 1)]
+        acc = {}
+        for nb in range(NB):
+            for e in range(E):
+                acc[nb, e] = psum.tile([P, 512], F32, name="acc%d%d" % (nb, e))
+        y = [keep.tile([P, S], F32, name="y%d" % nb) for nb in range(NB)]
+        ow = [keep.tile([P, T], F32, name="ow%d" % nb) for nb in range(NB)]
+
+        def cast(i):
+            c0 = (LAST - 1 - i) * T
+            if i == LAST:
+                nc.scalar.copy(planes[:], raw[i][:])
+            elif i < SPLIT:
+                nc.scalar.copy(win[:, c0 : c0 + H, :], raw[i, 0][:].rearrange("p e t -> p t e"))
+                nc.vector.tensor_copy(win[:, c0 + H : c0 + T, :], raw[i, 1][:].rearrange("p e t -> p t e"))
+            else:
+                nc.scalar.copy(win[:, c0 : c0 + T, :], raw[i][:].rearrange("p e t -> p t e"))
+
+        def gather(i, s0, s1):
+            g, u = divmod(i, 2)
+            c0 = (LAST - 1 - i) * T
+            width = T if i == 0 else 2 * T
+            if g < PASSES - 1:
+                dst = xg[g][:, u, s0:s1, :].rearrange("p s e -> p (s e)").bitcast(U32)
+            else:
+                dst = xi[g][:].rearrange("p s t -> p (s t)").bitcast(U32).rearrange("p (s u) -> p s u", u=2)[:, s0:s1, u]
+            nc.vector.tensor_copy(dst, winw[:, c0 : c0 + width].indirect(offs_t[:, s0 // 16 : s1 // 16]))
+
+        def weave(g):
+            src = xg[g][:].rearrange("p u s e -> p (u s e)").bitcast(I32).rearrange("p (u s) -> p s u", u=2)
+            dst = xi[g][:].rearrange("p s t -> p (s t)").bitcast(I32).rearrange("p (s u) -> p s u", u=2)
+            nc.vector.tensor_copy(dst, src)
+
+        def gather_scalar(s0, s1):
+            for e in range(2):
+                nc.scalar.activation(
+                    xi[PASSES - 1][:, s0:s1, 2 + e], planes[:, e, :].indirect(offs_t[:, s0 // 16 : s1 // 16]), COPY
+                )
+
+        def quant(g, s0, s1):
+            nc.vector.quantize_mx(
+                out=xc[:, g, s0:s1].bitcast(FP8X4),
+                scales=xs[:, g, s0:s1],
+                in_=xi[g][:, s0:s1, :].rearrange("p s t -> p (s t)"),
+            )
+
+        def mm(g, e):
+            cols = slice(e * C, (e + 1) * C)
+            for nb in range(NB):
+                feat = slice(nb * P, (nb + 1) * P)
+                nc.tensor.matmul_mx(
+                    out=acc[nb, e][:, 0:C],
+                    lhsT=wq[g][:, e, feat].bitcast(FP8X4),
+                    lhsT_scale=ws[:, e * PASSES + g, feat],
+                    rhs=xc[:, g, cols].bitcast(FP8X4),
+                    rhs_scale=xs[:, g, cols],
+                    start=(g == 0),
+                    stop=(g == PASSES - 1),
+                )
+
+        def evac(nb, e):
+            nc.scalar.copy(y[nb][:, e * C : (e + 1) * C], acc[nb, e][:, 0:C])
+
+        def scatter(nb, e):
+            cols = slice(e * C, (e + 1) * C)
+            nc.vector.tensor_tensor(
+                ow[nb][:].indirect(offs_t[:, e * (C // 16) : (e + 1) * (C // 16)]), y[nb][:, cols], gt[nb][:, cols], MULT
+            )
+
+        cast(0)
+        gather(0, 0, C)
+        gather(0, C, S)
+        cast(1)
+        gather(1, 0, S)
+        for g in range(1, PASSES - 1):
+            cast(2 * g)
+            weave(g - 1)
+            gather(2 * g, 0, S)
+            quant(g - 1, 0, S)
+            mm(g - 1, 0)
+            mm(g - 1, 1)
+            cast(2 * g + 1)
+            gather(2 * g + 1, 0, S)
+        g = PASSES - 1
+        cast(2 * g)
+        cast(2 * g + 1)
+        gather_scalar(0, C)
+        gather_scalar(C, S)
+        weave(g - 1)
+        gather(2 * g, 0, C)
+        quant(g - 1, 0, C)
+        mm(g - 1, 0)
+        quant(g, 0, C)
+        mm(g, 0)
+        gather(2 * g, C, S)
+        quant(g - 1, C, S)
+        mm(g - 1, 1)
+        quant(g, C, S)
+        mm(g, 1)
+        for e in range(E):
+            for nb in range(NB):
+                evac(nb, e)
+        scatter(0, 0)
+        scatter(1, 0)
+        scatter(0, 1)
+        nc.sync.dma_start(out[0:P, :], ow[0][:])
+        scatter(1, 1)
+        nc.sync.dma_start(out[P : 2 * P, :], ow[1][:])

@@ -13,6 +13,7 @@ U16 = mybir.dt.uint16
 U8 = mybir.dt.uint8
 FP8X4 = mybir.dt.float8_e4m3fn_x4
 MULT = mybir.AluOpType.mult
+ADD = mybir.AluOpType.add
 COPY = mybir.ActivationFunctionType.Copy
 
 P = 128
@@ -60,10 +61,10 @@ def tile_routed_moe_kernel(tc, xT, w_words, w_scales, gate, offs, out):
             nc.sync.dma_start(ws[r:P:32, :, :].bitcast(I32), sv[r].bitcast(I32))
 
         wq = []
-        for a in range(PASSES):
-            wq_a = keep.tile([P, E, N], I32, name="wq%d" % a, align_bytes=64)
-            nc.sync.dma_start(wq_a[:], w_words[:, a].rearrange("e p n r -> p e (n r)").bitcast(I32))
-            wq.append(wq_a)
+        for e in range(E):
+            wq_e = keep.tile([P, PASSES, N], I32, name="wq%d" % e, align_bytes=64)
+            nc.sync.dma_start(wq_e[:], w_words[e].rearrange("a p n r -> p a (n r)").bitcast(I32))
+            wq.append(wq_e)
 
         gt = []
         for nb in range(NB):
@@ -71,9 +72,9 @@ def tile_routed_moe_kernel(tc, xT, w_words, w_scales, gate, offs, out):
             nc.sync.dma_start(gt_nb[:], gate[nb * P : (nb + 1) * P, :])
             gt.append(gt_nb)
 
-        xc = keep.tile([P, PASSES, S], U32, name="xc", align_bytes=64)
-        xs = keep.tile([P, PASSES, S], U8, name="xs", align_bytes=64)
-        xi = [keep.tile([P, S, 4], BF16, name="xi%d" % g, align_bytes=64) for g in range(PASSES)]
+        xc = keep.tile([P, E, PASSES, C], U32, name="xc", align_bytes=64)
+        xs = keep.tile([P, E, PASSES, C], U8, name="xs", align_bytes=64)
+        xi = [keep.tile([P, E, 2, C, 4], BF16, name="xi%d" % h, align_bytes=64) for h in range(2)]
         win = keep.tile([P, LAST * T, 2], BF16, name="win", align_bytes=64)
         winw = win[:].rearrange("p t e -> p (t e)").bitcast(U32)
         planes = keep.tile([P, 2, T], BF16, name="planes", align_bytes=64)
@@ -91,9 +92,15 @@ def tile_routed_moe_kernel(tc, xT, w_words, w_scales, gate, offs, out):
                 nc.scalar.copy(planes[:], raw[i][:])
             elif i < SPLIT:
                 nc.scalar.copy(win[:, c0 : c0 + H, :], raw[i, 0][:].rearrange("p e t -> p t e"))
-                nc.vector.tensor_copy(win[:, c0 + H : c0 + T, :], raw[i, 1][:].rearrange("p e t -> p t e"))
+                if i == 0:
+                    nc.vector.tensor_copy(win[:, c0 + H : c0 + T, :], raw[i, 1][:].rearrange("p e t -> p t e"))
+                else:
+                    nc.scalar.copy(win[:, c0 + H : c0 + T, :], raw[i, 1][:].rearrange("p e t -> p t e"))
             else:
                 nc.scalar.copy(win[:, c0 : c0 + T, :], raw[i][:].rearrange("p e t -> p t e"))
+
+        def words(g):
+            return xi[g // 2][:, :, g % 2, :, :].rearrange("p e c t -> p e (c t)").bitcast(U32).rearrange("p e (c u) -> p e c u", u=2)
 
         def gather(i, s0, s1):
             g, u = divmod(i, 2)
@@ -102,40 +109,45 @@ def tile_routed_moe_kernel(tc, xT, w_words, w_scales, gate, offs, out):
             if g < PASSES - 1:
                 dst = xg[g][:, u, s0:s1, :].rearrange("p s e -> p (s e)").bitcast(U32)
             else:
-                dst = xi[g][:].rearrange("p s t -> p (s t)").bitcast(U32).rearrange("p (s u) -> p s u", u=2)[:, s0:s1, u]
+                dst = words(g)[:, :, :, u]
             nc.vector.tensor_copy(dst, winw[:, c0 : c0 + width].indirect(offs_t[:, s0 // 16 : s1 // 16]))
 
         def weave(g):
-            src = xg[g][:].rearrange("p u s e -> p (u s e)").bitcast(I32).rearrange("p (u s) -> p s u", u=2)
-            dst = xi[g][:].rearrange("p s t -> p (s t)").bitcast(I32).rearrange("p (s u) -> p s u", u=2)
+            src = xg[g][:].rearrange("p u s e -> p (u s e)").bitcast(I32).rearrange("p (u e c) -> p e c u", u=2, e=E)
+            dst = xi[g // 2][:, :, g % 2, :, :].rearrange("p e c t -> p e (c t)").bitcast(I32).rearrange("p e (c u) -> p e c u", u=2)
             nc.vector.tensor_copy(dst, src)
 
-        def gather_scalar(s0, s1):
-            for e in range(2):
+        def weave_gpsimd(g, e):
+            src = xg[g][:, :, e * C : (e + 1) * C, :].rearrange("p u s k -> p s u k")
+            dst = xi[g // 2][:, e, g % 2, :, :].rearrange("p s (u k) -> p s u k", u=2)
+            nc.gpsimd.tensor_scalar(dst, src, 1.0, 0.0, MULT, ADD)
+
+        def gather_scalar(e):
+            for k in range(2):
                 nc.scalar.activation(
-                    xi[PASSES - 1][:, s0:s1, 2 + e], planes[:, e, :].indirect(offs_t[:, s0 // 16 : s1 // 16]), COPY
+                    xi[1][:, e, 1, :, 2 + k], planes[:, k, :].indirect(offs_t[:, e * (C // 16) : (e + 1) * (C // 16)]), COPY
                 )
 
-        def quant(g, s0, s1):
+        def quant(h, e):
             nc.vector.quantize_mx(
-                out=xc[:, g, s0:s1].bitcast(FP8X4),
-                scales=xs[:, g, s0:s1],
-                in_=xi[g][:, s0:s1, :].rearrange("p s t -> p (s t)"),
+                out=xc[:, e, 2 * h : 2 * h + 2, :].rearrange("p g c -> p (g c)").bitcast(FP8X4),
+                scales=xs[:, e, 2 * h : 2 * h + 2, :].rearrange("p g c -> p (g c)"),
+                in_=xi[h][:, e, :, :, :].rearrange("p g c t -> p (g c t)"),
             )
 
-        def mm(g, e):
-            cols = slice(e * C, (e + 1) * C)
+        def mm(h, e):
             for nb in range(NB):
                 feat = slice(nb * P, (nb + 1) * P)
-                nc.tensor.matmul_mx(
-                    out=acc[nb, e][:, 0:C],
-                    lhsT=wq[g][:, e, feat].bitcast(FP8X4),
-                    lhsT_scale=ws[:, e * PASSES + g, feat],
-                    rhs=xc[:, g, cols].bitcast(FP8X4),
-                    rhs_scale=xs[:, g, cols],
-                    start=(g == 0),
-                    stop=(g == PASSES - 1),
-                )
+                for g in (2 * h, 2 * h + 1):
+                    nc.tensor.matmul_mx(
+                        out=acc[nb, e][:, 0:C],
+                        lhsT=wq[e][:, g, feat].bitcast(FP8X4),
+                        lhsT_scale=ws[:, e * PASSES + g, feat],
+                        rhs=xc[:, e, g, :].bitcast(FP8X4),
+                        rhs_scale=xs[:, e, g, :],
+                        start=(g == 0),
+                        stop=(g == PASSES - 1),
+                    )
 
         def evac(nb, e):
             nc.scalar.copy(y[nb][:, e * C : (e + 1) * C], acc[nb, e][:, 0:C])
@@ -151,31 +163,30 @@ def tile_routed_moe_kernel(tc, xT, w_words, w_scales, gate, offs, out):
         gather(0, C, S)
         cast(1)
         gather(1, 0, S)
-        for g in range(1, PASSES - 1):
-            cast(2 * g)
-            weave(g - 1)
-            gather(2 * g, 0, S)
-            quant(g - 1, 0, S)
-            mm(g - 1, 0)
-            mm(g - 1, 1)
-            cast(2 * g + 1)
-            gather(2 * g + 1, 0, S)
-        g = PASSES - 1
-        cast(2 * g)
-        cast(2 * g + 1)
-        gather_scalar(0, C)
-        gather_scalar(C, S)
-        weave(g - 1)
-        gather(2 * g, 0, C)
-        quant(g - 1, 0, C)
-        mm(g - 1, 0)
-        quant(g, 0, C)
-        mm(g, 0)
-        gather(2 * g, C, S)
-        quant(g - 1, C, S)
-        mm(g - 1, 1)
-        quant(g, C, S)
-        mm(g, 1)
+        weave_gpsimd(0, 0)
+        weave_gpsimd(0, 1)
+        cast(2)
+        gather(2, 0, S)
+        cast(3)
+        gather(3, 0, S)
+        weave_gpsimd(1, 1)
+        weave_gpsimd(1, 0)
+        cast(4)
+        gather(4, 0, S)
+        cast(5)
+        gather(5, 0, S)
+        cast(6)
+        cast(7)
+        gather_scalar(0)
+        gather_scalar(1)
+        for e in range(E):
+            quant(0, e)
+            mm(0, e)
+        gather(6, 0, S)
+        weave(2)
+        for e in range(E):
+            quant(1, e)
+            mm(1, e)
         for e in range(E):
             for nb in range(NB):
                 evac(nb, e)

@@ -43,8 +43,9 @@ def tile_routed_moe_kernel(tc, xT, w_words, w_scales, gate, offs, out):
         xv = xT.rearrange("(g p t) n -> g p t n", p=P, t=4)
         SPLIT = 2
         LAST = UNITS - 1
+        SEQ = [0, 1, 2, 3, 4, 6, 5, 7]
         raw = {}
-        for i in range(UNITS):
+        for i in SEQ:
             g, u = divmod(i, 2)
             if i < SPLIT:
                 for b in range(2):
@@ -72,8 +73,8 @@ def tile_routed_moe_kernel(tc, xT, w_words, w_scales, gate, offs, out):
             nc.sync.dma_start(gt_nb[:], gate[nb * P : (nb + 1) * P, :])
             gt.append(gt_nb)
 
-        xc = keep.tile([P, E, PASSES, C], U32, name="xc", align_bytes=64)
-        xs = keep.tile([P, E, PASSES, C], U8, name="xs", align_bytes=64)
+        xc = keep.tile([P, 2, E, 2, C], U32, name="xc", align_bytes=64)
+        xs = keep.tile([P, 2, E, 2, C], U8, name="xs", align_bytes=64)
         xi = [keep.tile([P, E, 2, C, 4], BF16, name="xi%d" % h, align_bytes=64) for h in range(2)]
         win = keep.tile([P, LAST * T, 2], BF16, name="win", align_bytes=64)
         winw = win[:].rearrange("p t e -> p (t e)").bitcast(U32)
@@ -87,7 +88,7 @@ def tile_routed_moe_kernel(tc, xT, w_words, w_scales, gate, offs, out):
         ow = [keep.tile([P, T], F32, name="ow%d" % nb) for nb in range(NB)]
 
         def cast(i):
-            c0 = (LAST - 1 - i) * T
+            c0 = (LAST - 1 - SEQ.index(i)) * T
             if i == LAST:
                 nc.scalar.copy(planes[:], raw[i][:])
             elif i < SPLIT:
@@ -104,7 +105,7 @@ def tile_routed_moe_kernel(tc, xT, w_words, w_scales, gate, offs, out):
 
         def gather(i, s0, s1):
             g, u = divmod(i, 2)
-            c0 = (LAST - 1 - i) * T
+            c0 = (LAST - 1 - SEQ.index(i)) * T
             width = T if i == 0 else 2 * T
             if g < PASSES - 1:
                 dst = xg[g][:, u, s0:s1, :].rearrange("p s e -> p (s e)").bitcast(U32)
@@ -128,10 +129,17 @@ def tile_routed_moe_kernel(tc, xT, w_words, w_scales, gate, offs, out):
                     xi[1][:, e, 1, :, 2 + k], planes[:, k, :].indirect(offs_t[:, e * (C // 16) : (e + 1) * (C // 16)]), COPY
                 )
 
+        def quant_both(h):
+            nc.vector.quantize_mx(
+                out=xc[:, h, :, :, :].rearrange("p e g c -> p (e g c)").bitcast(FP8X4),
+                scales=xs[:, h, :, :, :].rearrange("p e g c -> p (e g c)"),
+                in_=xi[h][:].rearrange("p e g c t -> p (e g c t)"),
+            )
+
         def quant(h, e):
             nc.vector.quantize_mx(
-                out=xc[:, e, 2 * h : 2 * h + 2, :].rearrange("p g c -> p (g c)").bitcast(FP8X4),
-                scales=xs[:, e, 2 * h : 2 * h + 2, :].rearrange("p g c -> p (g c)"),
+                out=xc[:, h, e, :, :].rearrange("p g c -> p (g c)").bitcast(FP8X4),
+                scales=xs[:, h, e, :, :].rearrange("p g c -> p (g c)"),
                 in_=xi[h][:, e, :, :, :].rearrange("p g c t -> p (g c t)"),
             )
 
@@ -143,8 +151,8 @@ def tile_routed_moe_kernel(tc, xT, w_words, w_scales, gate, offs, out):
                         out=acc[nb, e][:, 0:C],
                         lhsT=wq[e][:, g, feat].bitcast(FP8X4),
                         lhsT_scale=ws[:, e * PASSES + g, feat],
-                        rhs=xc[:, e, g, :].bitcast(FP8X4),
-                        rhs_scale=xs[:, e, g, :],
+                        rhs=xc[:, h, e, g % 2, :].bitcast(FP8X4),
+                        rhs_scale=xs[:, h, e, g % 2, :],
                         start=(g == 0),
                         stop=(g == PASSES - 1),
                     )
@@ -173,16 +181,16 @@ def tile_routed_moe_kernel(tc, xT, w_words, w_scales, gate, offs, out):
         weave_gpsimd(1, 0)
         cast(4)
         gather(4, 0, S)
+        cast(6)
+        gather(6, 0, S)
         cast(5)
         gather(5, 0, S)
-        cast(6)
         cast(7)
         gather_scalar(0)
         gather_scalar(1)
-        for e in range(E):
-            quant(0, e)
-            mm(0, e)
-        gather(6, 0, S)
+        quant_both(0)
+        mm(0, 0)
+        mm(0, 1)
         weave(2)
         for e in range(E):
             quant(1, e)

@@ -73,9 +73,12 @@ def tile_routed_moe_kernel(tc, xT, w_words, w_scales, gate, offs, out):
             nc.sync.dma_start(gt_nb[:], gate[nb * P : (nb + 1) * P, :])
             gt.append(gt_nb)
 
-        xc = keep.tile([P, 2, E, 2, C], U32, name="xc", align_bytes=64)
-        xs = keep.tile([P, 2, E, 2, C], U8, name="xs", align_bytes=64)
-        xi = [keep.tile([P, E, 2, C, 4], BF16, name="xi%d" % h, align_bytes=64) for h in range(2)]
+        xi_a = keep.tile([P, 2, S, 4], BF16, name="xi_a", align_bytes=64)
+        xc_a = keep.tile([P, 2, S], U32, name="xc_a", align_bytes=64)
+        xs_a = keep.tile([P, 2, S], U8, name="xs_a", align_bytes=64)
+        xi_b = keep.tile([P, E, 2, C, 4], BF16, name="xi_b", align_bytes=64)
+        xc_b = keep.tile([P, E, 2, C], U32, name="xc_b", align_bytes=64)
+        xs_b = keep.tile([P, E, 2, C], U8, name="xs_b", align_bytes=64)
         win = keep.tile([P, LAST * T, 2], BF16, name="win", align_bytes=64)
         winw = win[:].rearrange("p t e -> p (t e)").bitcast(U32)
         planes = keep.tile([P, 2, T], BF16, name="planes", align_bytes=64)
@@ -101,7 +104,7 @@ def tile_routed_moe_kernel(tc, xT, w_words, w_scales, gate, offs, out):
                 nc.scalar.copy(win[:, c0 : c0 + T, :], raw[i][:].rearrange("p e t -> p t e"))
 
         def words(g):
-            return xi[g // 2][:, :, g % 2, :, :].rearrange("p e c t -> p e (c t)").bitcast(U32).rearrange("p e (c u) -> p e c u", u=2)
+            return xi_b[:, :, g % 2, :, :].rearrange("p e c t -> p e (c t)").bitcast(U32).rearrange("p e (c u) -> p e c u", u=2)
 
         def gather(i, s0, s1):
             g, u = divmod(i, 2)
@@ -115,32 +118,32 @@ def tile_routed_moe_kernel(tc, xT, w_words, w_scales, gate, offs, out):
 
         def weave(g):
             src = xg[g][:].rearrange("p u s e -> p (u s e)").bitcast(I32).rearrange("p (u e c) -> p e c u", u=2, e=E)
-            dst = xi[g // 2][:, :, g % 2, :, :].rearrange("p e c t -> p e (c t)").bitcast(I32).rearrange("p e (c u) -> p e c u", u=2)
+            dst = xi_b[:, :, g % 2, :, :].rearrange("p e c t -> p e (c t)").bitcast(I32).rearrange("p e (c u) -> p e c u", u=2)
             nc.vector.tensor_copy(dst, src)
 
-        def weave_gpsimd(g, e):
-            src = xg[g][:, :, e * C : (e + 1) * C, :].rearrange("p u s k -> p s u k")
-            dst = xi[g // 2][:, e, g % 2, :, :].rearrange("p s (u k) -> p s u k", u=2)
+        def weave_gpsimd(g):
+            src = xg[g][:].rearrange("p u s k -> p s u k")
+            dst = xi_a[:, g, :, :].rearrange("p s (u k) -> p s u k", u=2)
             nc.gpsimd.tensor_scalar(dst, src, 1.0, 0.0, MULT, ADD)
 
         def gather_scalar(e):
             for k in range(2):
                 nc.scalar.activation(
-                    xi[1][:, e, 1, :, 2 + k], planes[:, k, :].indirect(offs_t[:, e * (C // 16) : (e + 1) * (C // 16)]), COPY
+                    xi_b[:, e, 1, :, 2 + k], planes[:, k, :].indirect(offs_t[:, e * (C // 16) : (e + 1) * (C // 16)]), COPY
                 )
 
-        def quant_both(h):
+        def quant_a():
             nc.vector.quantize_mx(
-                out=xc[:, h, :, :, :].rearrange("p e g c -> p (e g c)").bitcast(FP8X4),
-                scales=xs[:, h, :, :, :].rearrange("p e g c -> p (e g c)"),
-                in_=xi[h][:].rearrange("p e g c t -> p (e g c t)"),
+                out=xc_a[:].rearrange("p g s -> p (g s)").bitcast(FP8X4),
+                scales=xs_a[:].rearrange("p g s -> p (g s)"),
+                in_=xi_a[:].rearrange("p g s t -> p (g s t)"),
             )
 
-        def quant(h, e):
+        def quant_b(e):
             nc.vector.quantize_mx(
-                out=xc[:, h, e, :, :].rearrange("p g c -> p (g c)").bitcast(FP8X4),
-                scales=xs[:, h, e, :, :].rearrange("p g c -> p (g c)"),
-                in_=xi[h][:, e, :, :, :].rearrange("p g c t -> p (g c t)"),
+                out=xc_b[:, e, :, :].rearrange("p g c -> p (g c)").bitcast(FP8X4),
+                scales=xs_b[:, e, :, :].rearrange("p g c -> p (g c)"),
+                in_=xi_b[:, e, :, :, :].rearrange("p g c t -> p (g c t)"),
             )
 
         def mm(h, e):
@@ -151,8 +154,8 @@ def tile_routed_moe_kernel(tc, xT, w_words, w_scales, gate, offs, out):
                         out=acc[nb, e][:, 0:C],
                         lhsT=wq[e][:, g, feat].bitcast(FP8X4),
                         lhsT_scale=ws[:, e * PASSES + g, feat],
-                        rhs=xc[:, h, e, g % 2, :].bitcast(FP8X4),
-                        rhs_scale=xs[:, h, e, g % 2, :],
+                        rhs=(xc_a[:, g, e * C : (e + 1) * C] if h == 0 else xc_b[:, e, g % 2, :]).bitcast(FP8X4),
+                        rhs_scale=(xs_a[:, g, e * C : (e + 1) * C] if h == 0 else xs_b[:, e, g % 2, :]),
                         start=(g == 0),
                         stop=(g == PASSES - 1),
                     )
@@ -171,14 +174,12 @@ def tile_routed_moe_kernel(tc, xT, w_words, w_scales, gate, offs, out):
         gather(0, C, S)
         cast(1)
         gather(1, 0, S)
-        weave_gpsimd(0, 0)
-        weave_gpsimd(0, 1)
+        weave_gpsimd(0)
         cast(2)
         gather(2, 0, S)
         cast(3)
         gather(3, 0, S)
-        weave_gpsimd(1, 1)
-        weave_gpsimd(1, 0)
+        weave_gpsimd(1)
         cast(4)
         gather(4, 0, S)
         cast(6)
@@ -188,12 +189,12 @@ def tile_routed_moe_kernel(tc, xT, w_words, w_scales, gate, offs, out):
         cast(7)
         gather_scalar(0)
         gather_scalar(1)
-        quant_both(0)
+        quant_a()
         mm(0, 0)
         mm(0, 1)
         weave(2)
         for e in range(E):
-            quant(1, e)
+            quant_b(e)
             mm(1, e)
         for e in range(E):
             for nb in range(NB):

@@ -73,9 +73,9 @@ def tile_routed_moe_kernel(tc, xT, w_words, w_scales, gate, offs, out):
             nc.sync.dma_start(gt_nb[:], gate[nb * P : (nb + 1) * P, :])
             gt.append(gt_nb)
 
-        xi_a = keep.tile([P, 2, S, 4], BF16, name="xi_a", align_bytes=64)
-        xc_a = keep.tile([P, 2, S], U32, name="xc_a", align_bytes=64)
-        xs_a = keep.tile([P, 2, S], U8, name="xs_a", align_bytes=64)
+        xi_a = keep.tile([P, E, 2, C, 4], BF16, name="xi_a", align_bytes=64)
+        xc_a = keep.tile([P, E, 2, C], U32, name="xc_a", align_bytes=64)
+        xs_a = keep.tile([P, E, 2, C], U8, name="xs_a", align_bytes=64)
         xi_b = keep.tile([P, E, 2, C, 4], BF16, name="xi_b", align_bytes=64)
         xc_b = keep.tile([P, E, 2, C], U32, name="xc_b", align_bytes=64)
         xs_b = keep.tile([P, E, 2, C], U8, name="xs_b", align_bytes=64)
@@ -116,14 +116,14 @@ def tile_routed_moe_kernel(tc, xT, w_words, w_scales, gate, offs, out):
                 dst = words(g)[:, :, :, u]
             nc.vector.tensor_copy(dst, winw[:, c0 : c0 + width].indirect(offs_t[:, s0 // 16 : s1 // 16]))
 
-        def weave(g):
+        def weave(g, e):
             src = xg[g][:].rearrange("p u s e -> p (u s e)").bitcast(I32).rearrange("p (u e c) -> p e c u", u=2, e=E)
             dst = xi_b[:, :, g % 2, :, :].rearrange("p e c t -> p e (c t)").bitcast(I32).rearrange("p e (c u) -> p e c u", u=2)
-            nc.vector.tensor_copy(dst, src)
+            nc.vector.tensor_copy(dst[:, e, :, :], src[:, e, :, :])
 
         def weave_gpsimd(g):
-            src = xg[g][:].rearrange("p u s k -> p s u k")
-            dst = xi_a[:, g, :, :].rearrange("p s (u k) -> p s u k", u=2)
+            src = xg[g][:].rearrange("p u (e c) k -> p e c u k", e=E)
+            dst = xi_a[:, :, g, :, :].rearrange("p e c (u k) -> p e c u k", u=2)
             nc.gpsimd.tensor_scalar(dst, src, 1.0, 0.0, MULT, ADD)
 
         def gather_scalar(e):
@@ -132,11 +132,11 @@ def tile_routed_moe_kernel(tc, xT, w_words, w_scales, gate, offs, out):
                     xi_b[:, e, 1, :, 2 + k], planes[:, k, :].indirect(offs_t[:, e * (C // 16) : (e + 1) * (C // 16)]), COPY
                 )
 
-        def quant_a():
+        def quant_a(e):
             nc.vector.quantize_mx(
-                out=xc_a[:].rearrange("p g s -> p (g s)").bitcast(FP8X4),
-                scales=xs_a[:].rearrange("p g s -> p (g s)"),
-                in_=xi_a[:].rearrange("p g s t -> p (g s t)"),
+                out=xc_a[:, e, :, :].rearrange("p g c -> p (g c)").bitcast(FP8X4),
+                scales=xs_a[:, e, :, :].rearrange("p g c -> p (g c)"),
+                in_=xi_a[:, e, :, :, :].rearrange("p g c t -> p (g c t)"),
             )
 
         def quant_b(e):
@@ -154,8 +154,8 @@ def tile_routed_moe_kernel(tc, xT, w_words, w_scales, gate, offs, out):
                         out=acc[nb, e][:, 0:C],
                         lhsT=wq[e][:, g, feat].bitcast(FP8X4),
                         lhsT_scale=ws[:, e * PASSES + g, feat],
-                        rhs=(xc_a[:, g, e * C : (e + 1) * C] if h == 0 else xc_b[:, e, g % 2, :]).bitcast(FP8X4),
-                        rhs_scale=(xs_a[:, g, e * C : (e + 1) * C] if h == 0 else xs_b[:, e, g % 2, :]),
+                        rhs=(xc_a if h == 0 else xc_b)[:, e, g % 2, :].bitcast(FP8X4),
+                        rhs_scale=(xs_a if h == 0 else xs_b)[:, e, g % 2, :],
                         start=(g == 0),
                         stop=(g == PASSES - 1),
                     )
@@ -189,13 +189,16 @@ def tile_routed_moe_kernel(tc, xT, w_words, w_scales, gate, offs, out):
         cast(7)
         gather_scalar(0)
         gather_scalar(1)
-        quant_a()
+        quant_a(0)
         mm(0, 0)
+        weave(2, 0)
+        weave(2, 1)
+        quant_b(0)
+        mm(1, 0)
+        quant_a(1)
         mm(0, 1)
-        weave(2)
-        for e in range(E):
-            quant_b(e)
-            mm(1, e)
+        quant_b(1)
+        mm(1, 1)
         for e in range(E):
             for nb in range(NB):
                 evac(nb, e)

@@ -139,26 +139,26 @@ def tile_routed_moe_kernel(tc, xT, w_words, w_scales, gate, offs, out):
                 in_=xi_a[:, e, :, :, :].rearrange("p g c t -> p (g c t)"),
             )
 
-        def quant_b(e):
+        def quant_b(g, e):
             nc.vector.quantize_mx(
-                out=xc_b[:, e, :, :].rearrange("p g c -> p (g c)").bitcast(FP8X4),
-                scales=xs_b[:, e, :, :].rearrange("p g c -> p (g c)"),
-                in_=xi_b[:, e, :, :, :].rearrange("p g c t -> p (g c t)"),
+                out=xc_b[:, e, g % 2, :].bitcast(FP8X4),
+                scales=xs_b[:, e, g % 2, :],
+                in_=xi_b[:, e, g % 2, :, :].rearrange("p c t -> p (c t)"),
             )
 
-        def mm(h, e):
+        def mm(g, e):
+            h = g // 2
             for nb in range(NB):
                 feat = slice(nb * P, (nb + 1) * P)
-                for g in (2 * h, 2 * h + 1):
-                    nc.tensor.matmul_mx(
-                        out=acc[nb, e][:, 0:C],
-                        lhsT=wq[e][:, g, feat].bitcast(FP8X4),
-                        lhsT_scale=ws[:, e * PASSES + g, feat],
-                        rhs=(xc_a if h == 0 else xc_b)[:, e, g % 2, :].bitcast(FP8X4),
-                        rhs_scale=(xs_a if h == 0 else xs_b)[:, e, g % 2, :],
-                        start=(g == 0),
-                        stop=(g == PASSES - 1),
-                    )
+                nc.tensor.matmul_mx(
+                    out=acc[nb, e][:, 0:C],
+                    lhsT=wq[e][:, g, feat].bitcast(FP8X4),
+                    lhsT_scale=ws[:, e * PASSES + g, feat],
+                    rhs=(xc_a if h == 0 else xc_b)[:, e, g % 2, :].bitcast(FP8X4),
+                    rhs_scale=(xs_a if h == 0 else xs_b)[:, e, g % 2, :],
+                    start=(g == 0),
+                    stop=(g == PASSES - 1),
+                )
 
         def evac(nb, e):
             nc.scalar.copy(y[nb][:, e * C : (e + 1) * C], acc[nb, e][:, 0:C])
@@ -191,14 +191,20 @@ def tile_routed_moe_kernel(tc, xT, w_words, w_scales, gate, offs, out):
         gather_scalar(1)
         quant_a(0)
         mm(0, 0)
-        weave(2, 0)
-        weave(2, 1)
-        quant_b(0)
         mm(1, 0)
+        weave(2, 0)
+        quant_b(2, 0)
+        mm(2, 0)
+        weave(2, 1)
+        quant_b(3, 0)
+        mm(3, 0)
         quant_a(1)
         mm(0, 1)
-        quant_b(1)
         mm(1, 1)
+        quant_b(2, 1)
+        mm(2, 1)
+        quant_b(3, 1)
+        mm(3, 1)
         for e in range(E):
             for nb in range(NB):
                 evac(nb, e)

@@ -93,7 +93,8 @@ def tile_routed_moe_kernel(tc, xT, w_words, w_scales, gate, offs, out):
         def cast(i):
             c0 = (LAST - 1 - SEQ.index(i)) * T
             if i == LAST:
-                nc.scalar.copy(planes[:], raw[i][:])
+                nc.scalar.copy(planes[:, 0, :], raw[i][:, 0, :])
+                nc.gpsimd.tensor_scalar(planes[:, 1, :], raw[i][:, 1, :], 1.0, 0.0, MULT, ADD)
             elif i < SPLIT:
                 nc.scalar.copy(win[:, c0 : c0 + H, :], raw[i, 0][:].rearrange("p e t -> p t e"))
                 if i == 0:
@@ -126,11 +127,10 @@ def tile_routed_moe_kernel(tc, xT, w_words, w_scales, gate, offs, out):
             dst = xi_a[:, :, g, :, :].rearrange("p e c (u k) -> p e c u k", u=2)
             nc.gpsimd.tensor_scalar(dst, src, 1.0, 0.0, MULT, ADD)
 
-        def gather_scalar(e):
-            for k in range(2):
-                nc.scalar.activation(
-                    xi_b[:, e, 1, :, 2 + k], planes[:, k, :].indirect(offs_t[:, e * (C // 16) : (e + 1) * (C // 16)]), COPY
-                )
+        def gather_scalar(k, e):
+            nc.scalar.activation(
+                xi_b[:, e, 1, :, 2 + k], planes[:, k, :].indirect(offs_t[:, e * (C // 16) : (e + 1) * (C // 16)]), COPY
+            )
 
         def quant_a(e):
             nc.vector.quantize_mx(
@@ -187,8 +187,9 @@ def tile_routed_moe_kernel(tc, xT, w_words, w_scales, gate, offs, out):
         cast(5)
         gather(5, 0, S)
         cast(7)
-        gather_scalar(0)
-        gather_scalar(1)
+        for k in range(2):
+            for e in range(E):
+                gather_scalar(k, e)
         quant_a(0)
         mm(0, 0)
         mm(1, 0)

@@ -47,15 +47,10 @@ def tile_routed_moe_kernel(tc, xT, w_words, w_scales, gate, offs, out):
         raw = {}
         for i in SEQ:
             g, u = divmod(i, 2)
-            if i < SPLIT:
-                for b in range(2):
-                    raw[i, b] = keep.tile([P, 2, H], F32, name="raw%d_%d" % (i, b))
-                    nc.sync.dma_start(raw[i, b][:], xv[g, :, 2 * u : 2 * u + 2, b * H : (b + 1) * H])
-                if i == 0:
-                    nc.sync.dma_start(offs_t[:], offs)
-            else:
-                raw[i] = keep.tile([P, 2, T], F32, name="raw%d" % i)
-                nc.sync.dma_start(raw[i][:], xv[g, :, 2 * u : 2 * u + 2, :])
+            raw[i] = keep.tile([P, 2, T], F32, name="raw%d" % i)
+            nc.sync.dma_start(raw[i][:], xv[g, :, 2 * u : 2 * u + 2, :])
+            if i == 0:
+                nc.sync.dma_start(offs_t[:], offs)
 
         sv = w_scales.rearrange("e a q n -> (e a) q n").rearrange("c (Q r) n -> r Q c n", r=4)
         for r in range(4):
@@ -96,11 +91,12 @@ def tile_routed_moe_kernel(tc, xT, w_words, w_scales, gate, offs, out):
                 nc.scalar.copy(planes[:, 0, :], raw[i][:, 0, :])
                 nc.gpsimd.tensor_scalar(planes[:, 1, :], raw[i][:, 1, :], 1.0, 0.0, MULT, ADD)
             elif i < SPLIT:
-                nc.scalar.copy(win[:, c0 : c0 + H, :], raw[i, 0][:].rearrange("p e t -> p t e"))
+                src = raw[i][:].rearrange("p e t -> p t e")
+                nc.scalar.copy(win[:, c0 : c0 + H, :], src[:, 0:H, :])
                 if i == 0:
-                    nc.vector.tensor_copy(win[:, c0 + H : c0 + T, :], raw[i, 1][:].rearrange("p e t -> p t e"))
+                    nc.vector.tensor_copy(win[:, c0 + H : c0 + T, :], src[:, H:T, :])
                 else:
-                    nc.scalar.copy(win[:, c0 + H : c0 + T, :], raw[i, 1][:].rearrange("p e t -> p t e"))
+                    nc.scalar.copy(win[:, c0 + H : c0 + T, :], src[:, H:T, :])
             else:
                 nc.scalar.copy(win[:, c0 : c0 + T, :], raw[i][:].rearrange("p e t -> p t e"))
 

from contextlib import ExitStack

import concourse.mybir as mybir

K, T, E, C, N = 2048, 512, 2, 256, 256
FLOPS = 2 * K * N * E * C

F32 = mybir.dt.float32
BF16 = mybir.dt.bfloat16
U32 = mybir.dt.uint32
I32 = mybir.dt.int32
U16 = mybir.dt.uint16
U8 = mybir.dt.uint8
FP8X4 = mybir.dt.float8_e4m3fn_x4
MULT = mybir.AluOpType.mult
ADD = mybir.AluOpType.add
COPY = mybir.ActivationFunctionType.Copy

P = 128
PASSES = K // 512
UNITS = 2 * PASSES
NB = N // P
S = E * C
H = T // 2


def tile_routed_moe_kernel(tc, xT, w_words, w_scales, gate, offs, out):
    nc = tc.nc
    with ExitStack() as ctx:
        keep = ctx.enter_context(tc.tile_pool(name="keep", bufs=1))
        psum = ctx.enter_context(tc.psum_pool(name="psum", bufs=1))

        offs_t = keep.tile([P, S // 16], U16, name="offs_t")

        warm_in = keep.tile([P, 1], F32, name="warm_in")
        warm_out = keep.tile([P, 1], F32, name="warm_out")
        nc.vector.memset(warm_in[:], 0.0)
        nc.scalar.activation(warm_out[:], warm_in[:], COPY)

        ws = keep.tile([P, E * PASSES, N], U8, name="ws", align_bytes=64)
        nc.vector.memset(ws[:].rearrange("p c n -> p (c n)").bitcast(I32), 0)

        xv = xT.rearrange("(g p t) n -> g p t n", p=P, t=4)
        SPLIT = 2
        LAST = UNITS - 1
        SEQ = [0, 1, 2, 3, 4, 6, 5, 7]
        raw = {}
        for i in SEQ:
            g, u = divmod(i, 2)
            raw[i] = keep.tile([P, 2, T], F32, name="raw%d" % i)
            nc.sync.dma_start(raw[i][:], xv[g, :, 2 * u : 2 * u + 2, :])
            if i == 0:
                nc.sync.dma_start(offs_t[:], offs)

        sv = w_scales.rearrange("e a q n -> (e a) q n").rearrange("c (Q r) n -> r Q c n", r=4)
        for r in range(4):
            nc.sync.dma_start(ws[r:P:32, :, :].bitcast(I32), sv[r].bitcast(I32))

        wq = []
        for e in range(E):
            wq_e = keep.tile([P, PASSES, N], I32, name="wq%d" % e, align_bytes=64)
            nc.sync.dma_start(wq_e[:], w_words[e].rearrange("a p n r -> p a (n r)").bitcast(I32))
            wq.append(wq_e)

        gt = []
        for nb in range(NB):
            gt_nb = keep.tile([P, S], F32, name="gt%d" % nb)
            nc.sync.dma_start(gt_nb[:], gate[nb * P : (nb + 1) * P, :])
            gt.append(gt_nb)

        xi_a = keep.tile([P, E, 2, C, 4], BF16, name="xi_a", align_bytes=64)
        xc_a = keep.tile([P, E, 2, C], U32, name="xc_a", align_bytes=64)
        xs_a = keep.tile([P, E, 2, C], U8, name="xs_a", align_bytes=64)
        xi_b = keep.tile([P, E, 2, C, 4], BF16, name="xi_b", align_bytes=64)
        xc_b = keep.tile([P, E, 2, C], U32, name="xc_b", align_bytes=64)
        xs_b = keep.tile([P, E, 2, C], U8, name="xs_b", align_bytes=64)
        win = keep.tile([P, LAST * T, 2], BF16, name="win", align_bytes=64)
        winw = win[:].rearrange("p t e -> p (t e)").bitcast(U32)
        planes = keep.tile([P, 2, T], BF16, name="planes", align_bytes=64)
        xg = [keep.tile([P, 2, S, 2], BF16, name="xg%d" % g, align_bytes=64) for g in range(PASSES - 1)]
        acc = {}
        for nb in range(NB):
            for e in range(E):
                acc[nb, e] = psum.tile([P, 512], F32, name="acc%d%d" % (nb, e))
        y = [keep.tile([P, S], F32, name="y%d" % nb) for nb in range(NB)]
        ow = [keep.tile([P, T], F32, name="ow%d" % nb) for nb in range(NB)]

        def cast(i):
            c0 = (LAST - 1 - SEQ.index(i)) * T
            if i == LAST:
                nc.scalar.copy(planes[:, 0, :], raw[i][:, 0, :])
                nc.gpsimd.tensor_scalar(planes[:, 1, :], raw[i][:, 1, :], 1.0, 0.0, MULT, ADD)
            elif i < SPLIT:
                src = raw[i][:].rearrange("p e t -> p t e")
                nc.scalar.copy(win[:, c0 : c0 + H, :], src[:, 0:H, :])
                if i == 0:
                    nc.vector.tensor_copy(win[:, c0 + H : c0 + T, :], src[:, H:T, :])
                else:
                    nc.scalar.copy(win[:, c0 + H : c0 + T, :], src[:, H:T, :])
            else:
                nc.scalar.copy(win[:, c0 : c0 + T, :], raw[i][:].rearrange("p e t -> p t e"))

        def words(g):
            return xi_b[:, :, g % 2, :, :].rearrange("p e c t -> p e (c t)").bitcast(U32).rearrange("p e (c u) -> p e c u", u=2)

        def gather(i, s0, s1):
            g, u = divmod(i, 2)
            c0 = (LAST - 1 - SEQ.index(i)) * T
            width = T if i == 0 else 2 * T
            if g < PASSES - 1:
                dst = xg[g][:, u, s0:s1, :].rearrange("p s e -> p (s e)").bitcast(U32)
            else:
                dst = words(g)[:, :, :, u]
            nc.vector.tensor_copy(dst, winw[:, c0 : c0 + width].indirect(offs_t[:, s0 // 16 : s1 // 16]))

        def weave(g, e):
            src = xg[g][:].rearrange("p u s e -> p (u s e)").bitcast(I32).rearrange("p (u e c) -> p e c u", u=2, e=E)
            dst = xi_b[:, :, g % 2, :, :].rearrange("p e c t -> p e (c t)").bitcast(I32).rearrange("p e (c u) -> p e c u", u=2)
            nc.vector.tensor_copy(dst[:, e, :, :], src[:, e, :, :])

        def weave_gpsimd(g):
            src = xg[g][:].rearrange("p u (e c) k -> p e c u k", e=E)
            dst = xi_a[:, :, g, :, :].rearrange("p e c (u k) -> p e c u k", u=2)
            nc.gpsimd.tensor_scalar(dst, src, 1.0, 0.0, MULT, ADD)

        def gather_scalar(k, e):
            nc.scalar.activation(
                xi_b[:, e, 1, :, 2 + k], planes[:, k, :].indirect(offs_t[:, e * (C // 16) : (e + 1) * (C // 16)]), COPY
            )

        def quant_a(e):
            nc.vector.quantize_mx(
                out=xc_a[:, e, :, :].rearrange("p g c -> p (g c)").bitcast(FP8X4),
                scales=xs_a[:, e, :, :].rearrange("p g c -> p (g c)"),
                in_=xi_a[:, e, :, :, :].rearrange("p g c t -> p (g c t)"),
            )

        def quant_b(g, e):
            nc.vector.quantize_mx(
                out=xc_b[:, e, g % 2, :].bitcast(FP8X4),
                scales=xs_b[:, e, g % 2, :],
                in_=xi_b[:, e, g % 2, :, :].rearrange("p c t -> p (c t)"),
            )

        def mm(g, e):
            h = g // 2
            for nb in range(NB):
                feat = slice(nb * P, (nb + 1) * P)
                nc.tensor.matmul_mx(
                    out=acc[nb, e][:, 0:C],
                    lhsT=wq[e][:, g, feat].bitcast(FP8X4),
                    lhsT_scale=ws[:, e * PASSES + g, feat],
                    rhs=(xc_a if h == 0 else xc_b)[:, e, g % 2, :].bitcast(FP8X4),
                    rhs_scale=(xs_a if h == 0 else xs_b)[:, e, g % 2, :],
                    start=(g == 0),
                    stop=(g == PASSES - 1),
                )

        def evac(nb, e):
            nc.scalar.copy(y[nb][:, e * C : (e + 1) * C], acc[nb, e][:, 0:C])

        def scatter(nb, e):
            cols = slice(e * C, (e + 1) * C)
            nc.vector.tensor_tensor(
                ow[nb][:].indirect(offs_t[:, e * (C // 16) : (e + 1) * (C // 16)]), y[nb][:, cols], gt[nb][:, cols], MULT
            )

        cast(0)
        gather(0, 0, C)
        gather(0, C, S)
        cast(1)
        gather(1, 0, S)
        weave_gpsimd(0)
        cast(2)
        gather(2, 0, S)
        cast(3)
        gather(3, 0, S)
        weave_gpsimd(1)
        cast(4)
        gather(4, 0, S)
        cast(6)
        gather(6, 0, S)
        cast(5)
        gather(5, 0, S)
        cast(7)
        for k in range(2):
            for e in range(E):
                gather_scalar(k, e)
        quant_a(0)
        mm(0, 0)
        mm(1, 0)
        weave(2, 0)
        quant_b(2, 0)
        mm(2, 0)
        weave(2, 1)
        quant_b(3, 0)
        mm(3, 0)
        quant_a(1)
        mm(0, 1)
        mm(1, 1)
        quant_b(2, 1)
        mm(2, 1)
        quant_b(3, 1)
        mm(3, 1)
        for e in range(E):
            for nb in range(NB):
                evac(nb, e)
        scatter(0, 0)
        scatter(1, 0)
        scatter(0, 1)
        nc.sync.dma_start(out[0:P, :], ow[0][:])
        scatter(1, 1)
        nc.sync.dma_start(out[P : 2 * P, :], ow[1][:])
